import numpy as np
import ml_dtypes


def mxq(x, axis, fmt="e4m3"):
    dtype, down = {"e4m3": (ml_dtypes.float8_e4m3fn, 7), "e5m2": (ml_dtypes.float8_e5m2, 14)}[fmt]
    v = np.moveaxis(np.asarray(x, np.float32).astype(ml_dtypes.bfloat16).astype(np.float64), axis, -1)
    blocks = v.reshape(v.shape[:-1] + (-1, 32))
    amax = np.abs(blocks).max(-1, keepdims=True)
    byte = np.maximum(np.where(amax > 0, np.frexp(amax)[1] - 1 + 127, 0) - down, 1)
    scale = np.exp2(byte - 127.0)
    codes = (blocks / scale).astype(np.float32).astype(dtype).astype(np.float64)
    return np.moveaxis((codes * scale).reshape(v.shape), -1, axis)


WIDE = False


def mx_kscale(k):
    if not WIDE:
        return np.ones(k)
    levels = np.array([30, -30])
    if k % 512:
        return np.exp2(np.random.permutation(np.resize(levels, k // 32))).repeat(32)
    a = np.empty((k // 512, 16))
    for p in range(k // 512):
        a[p, :8] = np.random.permutation(np.resize(levels, 8))
        for g in range(8):
            far = levels[np.abs(levels - a[p, g]) >= 10]
            a[p, g + 8] = far[np.random.randint(len(far))]
    return np.exp2(a.ravel()).repeat(32)


BF16 = ml_dtypes.bfloat16


def bf(x):
    return np.asarray(x, np.float32).astype(BF16)


def f64(x):
    return np.asarray(x).astype(np.float64)


E2M1 = np.array([0.0, 0.5, 1.0, 1.5, 2.0, 3.0, 4.0, 6.0, -0.0, -0.5, -1.0, -1.5, -2.0, -3.0, -4.0, -6.0])


def pack_weight(w, fmt):
    k, n = w.shape
    w = f64(bf(w)).reshape(k // 32, 32, n)
    amax = np.abs(w).max(1)
    if fmt == "e4m3":
        byte = np.frexp(amax)[1] - 1 + 127 - 7
    else:
        mant, ex = np.frexp(amax / 6.0)
        byte = np.where(mant > 0.5, ex, ex - 1) + 127
    byte = np.clip(np.where(amax > 0, byte, 1), 1, 254)
    scaled = (w * np.exp2(127.0 - byte)[:, None, :]).reshape(k, n).astype(np.float32)
    by_word = np.ascontiguousarray(scaled.reshape(k // 512, 128, 4, n).transpose(0, 1, 3, 2))
    if fmt == "e4m3":
        words = by_word.astype(ml_dtypes.float8_e4m3fn).view(np.uint8)
    else:
        c = by_word.astype(ml_dtypes.float4_e2m1fn).view(np.uint8) & 0xF
        words = c[..., 0::2] | (c[..., 1::2] << 4)
    return np.ascontiguousarray(words), np.ascontiguousarray(byte.astype(np.uint8).reshape(k // 512, 16, n))


def unpack_weight(words, scales, fmt):
    g, p, n, _ = words.shape
    if fmt == "e4m3":
        vals = np.ascontiguousarray(words).view(ml_dtypes.float8_e4m3fn).astype(np.float64)
    else:
        nib = np.empty((g, p, n, 4), np.uint8)
        nib[..., 0::2] = words & 0xF
        nib[..., 1::2] = words >> 4
        vals = E2M1[nib]
    vals = vals * np.repeat(np.exp2(scales.astype(np.float64) - 127.0), 8, axis=1)[..., None]
    return vals.transpose(0, 1, 3, 2).reshape(g * 512, n)
def pack4(w):
    words, scales = pack_weight(w, "e2m1")
    return words.reshape(words.shape[0], 128, -1), scales


def unpack4(words, scales):
    return unpack_weight(words.reshape(words.shape[0], 128, -1, 2), scales, "e2m1")


T, C, F, D, Q = 1024, 2048, 1024, 1536, 512


def setup_inputs():
    s, c, u = mx_kscale(C), mx_kscale(F), mx_kscale(T)
    w_words, w_scales = pack4(np.random.standard_normal((C, F)) / np.sqrt(C) / s[:, None] * c)
    return {"x": bf(np.random.standard_normal((T, C)) * s),
            "w_words": w_words,
            "w_scales": w_scales,
            "w_key": bf(np.random.standard_normal((F, D)) / np.sqrt(F) / c[:, None]),
            "b_key": bf(0.3 * np.random.standard_normal(D)),
            "emphasis": bf(np.random.uniform(0.5, 1.5, T) * u),
            "mix": bf(np.random.standard_normal((Q, T)) / np.sqrt(T) / u),
            "gain": bf((1 + 0.1 * np.random.standard_normal(F)) / c)}


def reference(x, w_words, w_scales, w_key, b_key, emphasis, mix, gain):
    w = unpack4(w_words, w_scales)
    z = mxq(f64(x), 1, "e4m3") @ w
    h = np.maximum(z, 0)
    keys = (mxq(h, 1, "e5m2") @ mxq(f64(w_key), 0, "e4m3")) + f64(b_key)
    v = h * f64(emphasis)[:, None]
    slots = (mxq(f64(mix), 1, "e4m3") @ mxq(v, 0, "e5m2")) * f64(gain)
    return keys, slots

@@ -1,0 +1,410 @@
+from contextlib import ExitStack
+
+import concourse.mybir as mybir
+from concourse.masks import make_identity
+
+T, C, F, D, Q = 1024, 2048, 1024, 1536, 512
+FLOPS = 2 * T * C * F + 2 * T * F * D + 2 * Q * T * F
+
+F32 = mybir.dt.float32
+BF16 = mybir.dt.bfloat16
+I32 = mybir.dt.int32
+U32 = mybir.dt.uint32
+U8 = mybir.dt.uint8
+E4M3 = mybir.dt.float8_e4m3fn_x4
+E5M2 = mybir.dt.float8_e5m2_x4
+E2M1 = mybir.dt.float4_e2m1fn_x4
+ALU = mybir.AluOpType
+RELU = mybir.ActivationFunctionType.Relu
+
+P = 128
+PACK = 4
+KP = P * PACK
+BANKS = 8
+
+
+def tile_text_image_bridge_s9_kernel(
+    tc, x, w_words, w_scales, w_key, b_key, emphasis, mix, gain, keys, slots
+):
+    nc = tc.nc
+    with ExitStack() as ctx:
+        keep = ctx.enter_context(tc.tile_pool(name="keep", bufs=1))
+        stage = ctx.enter_context(tc.tile_pool(name="stage", bufs=2))
+        psum = ctx.enter_context(tc.psum_pool(name="psum", bufs=1))
+        ctx.enter_context(tc.manual_schedule())
+
+        def kept(name, index, shape, dtype):
+            return keep.tile(shape, dtype, name="%s_%s" % (name, index), align_bytes=64)
+
+        free_banks = list(range(BANKS))
+
+        def take_bank():
+            number = free_banks.pop(0)
+            bank = psum.tile([P, KP], F32, name="bank%d" % number, tag="bank%d" % number)
+            return number, bank
+
+        def quantize(name, index, source, fmt):
+            width = source.shape[1] // PACK
+            codes = kept(name + "_codes", index, [P, width], U32)
+            scales = kept(name + "_scales", index, [P, width], U8)
+            nc.vector.quantize_mx(out=codes[:].bitcast(fmt), scales=scales[:], in_=source)
+            return codes, scales
+
+        def copy_on(engine, out, in_):
+            if engine == "scalar":
+                nc.scalar.copy(out=out, in_=in_)
+            else:
+                nc.vector.tensor_copy(out=out, in_=in_)
+
+        w_plane = [kept("w_plane", h, [P, 4, KP], U8) for h in range(2)]
+        warm = kept("warm", 0, [P, 8], F32)
+        nc.vector.memset(w_plane[0][:].bitcast(I32), 0)
+        nc.vector.memset(warm[:, 0:4], 0.0)
+        nc.vector.memset(w_plane[1][:].bitcast(I32), 0)
+        ident = kept("ident", 0, [P, P], F32)
+        make_identity(nc, ident[:])
+        nc.scalar.activation(out=warm[:, 4:8], in_=warm[:, 0:4], func=RELU)
+
+        x_sb, w_sb, wk_raw, mix_sb = {}, {}, {}, {}
+
+        def load_x(group, t, pieces=1):
+            x_sb[group, t] = kept("x", 4 * group + t, [P, C], BF16)
+            rows = x[group * KP : (group + 1) * KP, :].rearrange("(p t) k -> p t k", t=PACK)
+            step = C // pieces
+            for k0 in range(0, C, step):
+                nc.sync.dma_start(out=x_sb[group, t][:, k0 : k0 + step], in_=rows[:, t, k0 : k0 + step])
+
+        def load_w(h):
+            for quad in range(4):
+                nc.sync.dma_start(
+                    out=w_plane[h][32 * quad : 32 * quad + 4, :, :].bitcast(I32),
+                    in_=w_scales[:, 4 * quad : 4 * quad + 4, h * KP : (h + 1) * KP]
+                    .rearrange("g r n -> r g n")
+                    .bitcast(I32),
+                )
+            w_sb[h] = kept("w", h, [P, 4, 2 * KP], U8)
+            nc.sync.dma_start(
+                out=w_sb[h][:].bitcast(I32),
+                in_=w_words[:, :, 2 * h * KP : 2 * (h + 1) * KP].rearrange("g p n -> p g n").bitcast(I32),
+            )
+
+        def load_wk(g, j):
+            wk_raw[g, j] = kept("wk_raw", 3 * g + j, [P, PACK, KP], BF16)
+            nc.sync.dma_start(
+                out=wk_raw[g, j][:],
+                in_=w_key[g * KP : (g + 1) * KP, j * KP : (j + 1) * KP].rearrange("(p t) d -> p t d", t=PACK),
+            )
+
+        def load_mix(pair):
+            mix_sb[pair] = kept("mix", pair, [P, 2, T], BF16)
+            nc.sync.dma_start(
+                out=mix_sb[pair][:],
+                in_=mix[2 * pair * P : 2 * (pair + 1) * P, :].rearrange("(s p) k -> p s k", p=P),
+            )
+
+        emph = kept("emph", 0, [P, 2, PACK], BF16)
+        bias = kept("bias", 0, [P, D], BF16)
+        gains = kept("gains", 0, [P, F], BF16)
+
+        load_x(0, 0, pieces=2)
+        load_x(0, 1)
+        load_w(0)
+        load_x(0, 2)
+        load_x(0, 3)
+        nc.sync.dma_start(out=emph[:], in_=emphasis.rearrange("(g p t) -> p g t", g=2, t=PACK))
+        load_w(1)
+        load_wk(0, 0)
+        load_x(1, 0)
+        load_x(1, 1)
+        load_wk(1, 0)
+        load_wk(0, 1)
+        load_x(1, 2)
+        load_x(1, 3)
+        load_wk(1, 1)
+        load_wk(0, 2)
+        load_wk(1, 2)
+        nc.sync.dma_start(out=bias[:], in_=b_key.partition_broadcast(P))
+        load_mix(0)
+        load_mix(1)
+        nc.sync.dma_start(out=gains[:], in_=gain.partition_broadcast(P))
+
+        banks = {}
+        staged = {}
+        xq, hq, vq, wq, mq = {}, {}, {}, {}, {}
+
+        def x_turn(group, t, half):
+            number, bank = take_bank()
+            banks["x", group, t, half] = number, bank
+            words = x_sb[group, t][:].bitcast(F32)
+            for i in range(4):
+                g, u = 2 * half + i // 2, i % 2
+                nc.tensor.transpose(
+                    bank[:, i * P : (i + 1) * P], words[:, 256 * g + u : 256 * (g + 1) : 2], ident[:]
+                )
+
+        def turned_out(kind, index, half, engine):
+            number, bank = banks.pop((kind,) + index + (half,))
+            if half == 0:
+                staged[kind, index] = stage.tile(
+                    [P, 4 * KP], BF16, name="turned_" + kind, tag="turned", bufs=4, align_bytes=64
+                )
+            out = staged[kind, index][:, half * 2 * KP : (half + 1) * 2 * KP].bitcast(F32)
+            copy_on(
+                engine,
+                out.rearrange("p (a r u) -> p a r u", a=2, u=2),
+                bank[:].rearrange("p (a u r) -> p a r u", a=2, u=2),
+            )
+            free_banks.append(number)
+
+        def x_quant(group, t):
+            xq[group, t] = quantize("x", 4 * group + t, staged.pop(("x", (group, t)))[:], E4M3)
+
+        def z_open(group, c):
+            banks["z", group, c] = take_bank()
+
+        def z_passes(group, chunks, t):
+            codes, scales = xq[group, t]
+            for g in range(4):
+                for c in chunks:
+                    h, cc = divmod(c, 4)
+                    nc.tensor.matmul_mx(
+                        out=banks["z", group, c][1][:, t * P : (t + 1) * P],
+                        lhsT=codes[:, g * P : (g + 1) * P].bitcast(E4M3),
+                        lhsT_scale=scales[:, g * P : (g + 1) * P],
+                        rhs=w_sb[h][:, g, 2 * cc * P : 2 * (cc + 1) * P].bitcast(E2M1),
+                        rhs_scale=w_plane[h][:, g, cc * P : (cc + 1) * P],
+                        start=(g == 0),
+                        stop=(g == 3),
+                    )
+
+        def z_all(group, chunks):
+            for c in chunks:
+                z_open(group, c)
+            for t in range(PACK):
+                z_passes(group, chunks, t)
+
+        def z_out(group, c):
+            number, bank = banks.pop(("z", group, c))
+            h, cc = divmod(c, 4)
+            if cc == 0:
+                staged["h", group, h] = stage.tile([P, PACK, 2, 256], BF16, name="h_rows", bufs=3, align_bytes=64)
+                staged["v", group, h] = stage.tile([P, KP, PACK], BF16, name="v_rows", bufs=2, align_bytes=64)
+            nc.scalar.activation(
+                out=staged["h", group, h][:, :, :, 64 * cc : 64 * (cc + 1)].rearrange("p t u (m e) -> p u t m e", e=2),
+                in_=bank[:].rearrange("p (t m u e) -> p u t m e", t=PACK, u=2, e=2),
+                func=RELU,
+            )
+            nc.vector.scalar_tensor_tensor(
+                out=staged["v", group, h][:, cc * P : (cc + 1) * P, :],
+                in0=bank[:].rearrange("p (t f) -> p f t", t=PACK),
+                scalar=0.0,
+                in1=emph[:, group, :].unsqueeze(1).to_broadcast([P, P, PACK]),
+                op0=ALU.max,
+                op1=ALU.mult,
+            )
+            free_banks.append(number)
+
+        def v_quant(group, h):
+            rows = staged.pop(("v", group, h))
+            vq[group, h] = quantize("v", 2 * group + h, rows[:].rearrange("p f t -> p (f t)"), E5M2)
+
+        def h_turn(group, g, half):
+            number, bank = take_bank()
+            banks["h", group, g, half] = number, bank
+            words = staged["h", group, g][:].bitcast(F32)
+            for i in range(4):
+                nc.tensor.transpose(bank[:, i * P : (i + 1) * P], words[:, 2 * half + i // 2, i % 2, :], ident[:])
+
+        def h_quant(group, g):
+            hq[group, g] = quantize("h", 2 * group + g, staged.pop(("h", (group, g)))[:], E5M2)
+
+        def mix_turn(pair, half):
+            number, bank = take_bank()
+            banks["m", pair, half] = number, bank
+            words = mix_sb[pair][:, half, :].bitcast(F32)
+            for i in range(4):
+                group, u = i // 2, i % 2
+                nc.tensor.transpose(
+                    bank[:, i * P : (i + 1) * P], words[:, 256 * group + u : 256 * (group + 1) : 2], ident[:]
+                )
+
+        def mix_quant(pair):
+            mq[pair] = quantize("mix", pair, staged.pop(("m", (pair,)))[:], E4M3)
+
+        def wk_weave(g, j, engine):
+            staged["wk", g, j] = stage.tile([P, KP, PACK], BF16, name="wk_rows", bufs=2, align_bytes=64)
+            copy_on(
+                engine,
+                staged["wk", g, j][:].rearrange("p (c i) t -> p c t i", i=4),
+                wk_raw[g, j][:].rearrange("p t (c i) -> p c t i", i=4),
+            )
+
+        def wk_quant(g, j):
+            rows = staged.pop(("wk", g, j))
+            wq[g, j] = quantize("wk", 3 * g + j, rows[:].rearrange("p d t -> p (d t)"), E4M3)
+
+        def keys_pass(group, t, j, g):
+            if g == 0:
+                banks["k", group, t, j] = take_bank()
+            nc.tensor.matmul_mx(
+                out=banks["k", group, t, j][1][:],
+                lhsT=hq[group, g][0][:, t * P : (t + 1) * P].bitcast(E5M2),
+                lhsT_scale=hq[group, g][1][:, t * P : (t + 1) * P],
+                rhs=wq[g, j][0][:].bitcast(E4M3),
+                rhs_scale=wq[g, j][1][:],
+                start=(g == 0),
+                stop=(g == 1),
+            )
+
+        def keys_out(group, t, j):
+            number, bank = banks.pop(("k", group, t, j))
+            result = stage.tile([P, KP], F32, name="result", tag="result", bufs=10)
+            cols = slice(j * KP, (j + 1) * KP)
+            nc.vector.tensor_tensor(out=result[:], in0=bank[:], in1=bias[:, cols], op=ALU.add)
+            rows = keys[group * KP : (group + 1) * KP, :].rearrange("(p t) d -> p t d", t=PACK)
+            nc.sync.dma_start(out=rows[:, t, cols], in_=result[:])
+            free_banks.append(number)
+
+        def keys_both(group, t, j):
+            keys_pass(group, t, j, 0)
+            keys_pass(group, t, j, 1)
+
+        def slots_both(s, h):
+            banks["s", s, h] = take_bank()
+            codes, scales = mq[s // 2]
+            for group in range(2):
+                cols = slice((2 * (s % 2) + group) * P, (2 * (s % 2) + group + 1) * P)
+                nc.tensor.matmul_mx(
+                    out=banks["s", s, h][1][:],
+                    lhsT=codes[:, cols].bitcast(E4M3),
+                    lhsT_scale=scales[:, cols],
+                    rhs=vq[group, h][0][:].bitcast(E5M2),
+                    rhs_scale=vq[group, h][1][:],
+                    start=(group == 0),
+                    stop=(group == 1),
+                )
+
+        def slots_out(s, h):
+            number, bank = banks.pop(("s", s, h))
+            result = stage.tile([P, KP], F32, name="result", tag="result", bufs=10)
+            cols = slice(h * KP, (h + 1) * KP)
+            nc.vector.tensor_tensor(out=result[:], in0=bank[:], in1=gains[:, cols], op=ALU.mult)
+            nc.sync.dma_start(out=slots[s * P : (s + 1) * P, cols], in_=result[:])
+            free_banks.append(number)
+
+        def turn_pair(turn, *index):
+            turn(*index, 0)
+            turn(*index, 1)
+
+        def out_pair(kind, index, second="scalar"):
+            turned_out(kind, index, 0, "scalar")
+            turned_out(kind, index, 1, second)
+
+        def keys_run(group, j, ts):
+            for t in ts:
+                keys_both(group, t, j)
+                keys_out(group, t, j)
+
+        turn_pair(x_turn, 0, 0)
+        out_pair("x", (0, 0), "vector")
+        turn_pair(x_turn, 0, 1)
+        x_quant(0, 0)
+        out_pair("x", (0, 1), "vector")
+        for c in range(4):
+            z_open(0, c)
+        z_passes(0, range(4), 0)
+        x_quant(0, 1)
+        turn_pair(x_turn, 0, 2)
+        out_pair("x", (0, 2), "vector")
+        x_quant(0, 2)
+        turn_pair(x_turn, 0, 3)
+        z_passes(0, range(4), 1)
+        out_pair("x", (0, 3), "vector")
+        z_passes(0, range(4), 2)
+        x_quant(0, 3)
+        z_passes(0, [0, 1], 3)
+        z_passes(0, [2, 3], 3)
+
+        wk_weave(0, 0, "vector")
+        z_all(0, [4, 5])
+        for c in range(4):
+            z_out(0, c)
+        turn_pair(x_turn, 1, 0)
+        turn_pair(x_turn, 1, 1)
+        wk_quant(0, 0)
+        out_pair("x", (1, 0))
+        v_quant(0, 0)
+        wk_weave(1, 0, "vector")
+        x_quant(1, 0)
+        z_out(0, 4)
+        z_out(0, 5)
+        z_all(0, [6, 7])
+        out_pair("x", (1, 1))
+        wk_quant(1, 0)
+        wk_weave(0, 1, "vector")
+        x_quant(1, 1)
+        turn_pair(x_turn, 1, 2)
+        turn_pair(x_turn, 1, 3)
+        out_pair("x", (1, 2))
+        wk_quant(0, 1)
+        z_out(0, 6)
+        x_quant(1, 2)
+        out_pair("x", (1, 3))
+        z_out(0, 7)
+        turn_pair(h_turn, 0, 0)
+        x_quant(1, 3)
+        wk_weave(1, 1, "vector")
+        out_pair("h", (0, 0))
+        v_quant(0, 1)
+        z_all(1, [0, 1])
+        wk_quant(1, 1)
+        turn_pair(h_turn, 0, 1)
+        h_quant(0, 0)
+        out_pair("h", (0, 1))
+        z_out(1, 0)
+        h_quant(0, 1)
+        z_out(1, 1)
+        wk_weave(0, 2, "scalar")
+        z_all(1, [2, 3])
+        keys_run(0, 0, range(2))
+        z_out(1, 2)
+        z_out(1, 3)
+        keys_run(0, 0, range(2, 4))
+        wk_quant(0, 2)
+        wk_weave(1, 2, "scalar")
+        keys_run(0, 1, range(2))
+        v_quant(1, 0)
+        turn_pair(mix_turn, 0)
+        turn_pair(mix_turn, 1)
+        out_pair("m", (0,))
+        keys_run(0, 1, range(2, 4))
+        wk_quant(1, 2)
+        z_all(1, [4, 5])
+        mix_quant(0)
+        out_pair("m", (1,))
+        keys_run(0, 2, range(2))
+        mix_quant(1)
+        turn_pair(h_turn, 1, 0)
+        z_out(1, 4)
+        z_out(1, 5)
+        out_pair("h", (1, 0))
+        z_all(1, [6])
+        keys_run(0, 2, range(2, 4))
+        z_all(1, [7])
+        z_out(1, 6)
+        h_quant(1, 0)
+        z_out(1, 7)
+        for s in range(4):
+            slots_both(s, 0)
+            slots_out(s, 0)
+            if s == 1:
+                v_quant(1, 1)
+        turn_pair(h_turn, 1, 1)
+        out_pair("h", (1, 1))
+        for s in range(4):
+            slots_both(s, 1)
+            slots_out(s, 1)
+            if s == 1:
+                h_quant(1, 1)
+        for j in range(3):
+            keys_run(1, j, range(4))

@@ -88,12 +88,14 @@ def tile_text_image_bridge_s9_kernel(
                 in_=w_words[:, :, 2 * h * KP : 2 * (h + 1) * KP].rearrange("g p n -> p g n").bitcast(I32),
             )
 
-        def load_wk(g, j):
-            wk_raw[g, j] = kept("wk_raw", 3 * g + j, [P, PACK, KP], BF16)
+        def load_wk(g, first, last):
+            raw = kept("wk_raw", 3 * g + first, [P, PACK, (last - first) * KP], BF16)
             nc.sync.dma_start(
-                out=wk_raw[g, j][:],
-                in_=w_key[g * KP : (g + 1) * KP, j * KP : (j + 1) * KP].rearrange("(p t) d -> p t d", t=PACK),
+                out=raw[:],
+                in_=w_key[g * KP : (g + 1) * KP, first * KP : last * KP].rearrange("(p t) d -> p t d", t=PACK),
             )
+            for j in range(first, last):
+                wk_raw[g, j] = raw[:, :, (j - first) * KP : (j - first + 1) * KP]
 
         def load_mix(pair):
             mix_sb[pair] = kept("mix", pair, [P, 2, T], BF16)
@@ -101,6 +103,10 @@ def tile_text_image_bridge_s9_kernel(
                 out=mix_sb[pair][:],
                 in_=mix[2 * pair * P : 2 * (pair + 1) * P, :].rearrange("(s p) k -> p s k", p=P),
             )
+
+        def load_row(tile, row, j):
+            cols = slice(j * KP, (j + 1) * KP)
+            nc.sync.dma_start(out=tile[:, cols], in_=row[cols].partition_broadcast(P))
 
         emph = kept("emph", 0, [P, 2, PACK], BF16)
         bias = kept("bias", 0, [P, D], BF16)
@@ -111,35 +117,55 @@ def tile_text_image_bridge_s9_kernel(
         load_w(0)
         load_x(0, 2)
         load_x(0, 3)
-        nc.sync.dma_start(out=emph[:], in_=emphasis.rearrange("(g p t) -> p g t", g=2, t=PACK))
+        load_wk(0, 0, 1)
         load_w(1)
-        load_wk(0, 0)
         load_x(1, 0)
         load_x(1, 1)
-        load_wk(1, 0)
-        load_wk(0, 1)
-        load_x(1, 2)
+        nc.sync.dma_start(out=emph[:], in_=emphasis.rearrange("(g p t) -> p g t", g=2, t=PACK))
         load_x(1, 3)
-        load_wk(1, 1)
-        load_wk(0, 2)
-        load_wk(1, 2)
-        nc.sync.dma_start(out=bias[:], in_=b_key.partition_broadcast(P))
+        load_x(1, 2)
+        load_wk(1, 0, 1)
         load_mix(0)
         load_mix(1)
-        nc.sync.dma_start(out=gains[:], in_=gain.partition_broadcast(P))
+        load_row(bias, b_key, 0)
+        load_wk(0, 1, 3)
+        load_row(bias, b_key, 2)
+        load_wk(1, 1, 3)
+        load_row(gains, gain, 0)
+        load_row(gains, gain, 1)
+        load_row(bias, b_key, 1)
 
         banks = {}
         staged = {}
         xq, hq, vq, wq, mq = {}, {}, {}, {}, {}
 
+        parted = {}
+
+        def part(index, rows, engine):
+            parted[index] = stage.tile([P, 8, P], F32, name="parted", bufs=3, align_bytes=64)
+            copy_on(
+                engine,
+                parted[index][:].rearrange("p (a u) m -> p a u m", u=2),
+                rows.bitcast(F32).rearrange("p (a m u) -> p a u m", m=P, u=2),
+            )
+
+        def word_column(index, rows, i):
+            if index in parted:
+                return parted[index][:, i, :]
+            return rows.bitcast(F32)[:, 256 * (i // 2) + i % 2 : 256 * (i // 2 + 1) : 2]
+
+        def x_part(group, t, engine="scalar"):
+            part(("x", group, t), x_sb[group, t][:], engine)
+
+        def mix_part(pair, engine="scalar"):
+            part(("m", pair), mix_sb[pair][:].rearrange("p s k -> p (s k)"), engine)
+
         def x_turn(group, t, half):
             number, bank = take_bank()
             banks["x", group, t, half] = number, bank
-            words = x_sb[group, t][:].bitcast(F32)
             for i in range(4):
-                g, u = 2 * half + i // 2, i % 2
                 nc.tensor.transpose(
-                    bank[:, i * P : (i + 1) * P], words[:, 256 * g + u : 256 * (g + 1) : 2], ident[:]
+                    bank[:, i * P : (i + 1) * P], word_column(("x", group, t), x_sb[group, t][:], 4 * half + i), ident[:]
                 )
 
         def turned_out(kind, index, half, engine):
@@ -183,17 +209,30 @@ def tile_text_image_bridge_s9_kernel(
             for t in range(PACK):
                 z_passes(group, chunks, t)
 
-        def z_out(group, c):
-            number, bank = banks.pop(("z", group, c))
+        z_read = set()
+
+        def z_release(group, c):
+            if (group, c) in z_read:
+                free_banks.append(banks.pop(("z", group, c))[0])
+            z_read.add((group, c))
+
+        def h_out(group, c):
+            bank = banks["z", group, c][1]
             h, cc = divmod(c, 4)
             if cc == 0:
                 staged["h", group, h] = stage.tile([P, PACK, 2, 256], BF16, name="h_rows", bufs=3, align_bytes=64)
-                staged["v", group, h] = stage.tile([P, KP, PACK], BF16, name="v_rows", bufs=2, align_bytes=64)
             nc.scalar.activation(
                 out=staged["h", group, h][:, :, :, 64 * cc : 64 * (cc + 1)].rearrange("p t u (m e) -> p u t m e", e=2),
                 in_=bank[:].rearrange("p (t m u e) -> p u t m e", t=PACK, u=2, e=2),
                 func=RELU,
             )
+            z_release(group, c)
+
+        def v_out(group, c):
+            bank = banks["z", group, c][1]
+            h, cc = divmod(c, 4)
+            if cc == 0:
+                staged["v", group, h] = stage.tile([P, KP, PACK], BF16, name="v_rows", bufs=2, align_bytes=64)
             nc.vector.scalar_tensor_tensor(
                 out=staged["v", group, h][:, cc * P : (cc + 1) * P, :],
                 in0=bank[:].rearrange("p (t f) -> p f t", t=PACK),
@@ -202,7 +241,11 @@ def tile_text_image_bridge_s9_kernel(
                 op0=ALU.max,
                 op1=ALU.mult,
             )
-            free_banks.append(number)
+            z_release(group, c)
+
+        def z_out(group, c):
+            h_out(group, c)
+            v_out(group, c)
 
         def v_quant(group, h):
             rows = staged.pop(("v", group, h))
@@ -221,12 +264,8 @@ def tile_text_image_bridge_s9_kernel(
         def mix_turn(pair, half):
             number, bank = take_bank()
             banks["m", pair, half] = number, bank
-            words = mix_sb[pair][:, half, :].bitcast(F32)
             for i in range(4):
-                group, u = i // 2, i % 2
-                nc.tensor.transpose(
-                    bank[:, i * P : (i + 1) * P], words[:, 256 * group + u : 256 * (group + 1) : 2], ident[:]
-                )
+                nc.tensor.transpose(bank[:, i * P : (i + 1) * P], word_column(("m", pair), mix_sb[pair][:].rearrange("p s k -> p (s k)"), 4 * half + i), ident[:])
 
         def mix_quant(pair):
             mq[pair] = quantize("mix", pair, staged.pop(("m", (pair,)))[:], E4M3)
@@ -236,7 +275,7 @@ def tile_text_image_bridge_s9_kernel(
             copy_on(
                 engine,
                 staged["wk", g, j][:].rearrange("p (c i) t -> p c t i", i=4),
-                wk_raw[g, j][:].rearrange("p t (c i) -> p c t i", i=4),
+                wk_raw[g, j].rearrange("p t (c i) -> p c t i", i=4),
             )
 
         def wk_quant(g, j):
@@ -258,7 +297,7 @@ def tile_text_image_bridge_s9_kernel(
 
         def keys_out(group, t, j):
             number, bank = banks.pop(("k", group, t, j))
-            result = stage.tile([P, KP], F32, name="result", tag="result", bufs=10)
+            result = stage.tile([P, KP], F32, name="result", tag="result", bufs=12)
             cols = slice(j * KP, (j + 1) * KP)
             nc.vector.tensor_tensor(out=result[:], in0=bank[:], in1=bias[:, cols], op=ALU.add)
             rows = keys[group * KP : (group + 1) * KP, :].rearrange("(p t) d -> p t d", t=PACK)
@@ -286,125 +325,216 @@ def tile_text_image_bridge_s9_kernel(
 
         def slots_out(s, h):
             number, bank = banks.pop(("s", s, h))
-            result = stage.tile([P, KP], F32, name="result", tag="result", bufs=10)
+            result = stage.tile([P, KP], F32, name="result", tag="result", bufs=12)
             cols = slice(h * KP, (h + 1) * KP)
             nc.vector.tensor_tensor(out=result[:], in0=bank[:], in1=gains[:, cols], op=ALU.mult)
             nc.sync.dma_start(out=slots[s * P : (s + 1) * P, cols], in_=result[:])
             free_banks.append(number)
 
-        def turn_pair(turn, *index):
-            turn(*index, 0)
-            turn(*index, 1)
-
-        def out_pair(kind, index, second="scalar"):
-            turned_out(kind, index, 0, "scalar")
-            turned_out(kind, index, 1, second)
-
-        def keys_run(group, j, ts):
-            for t in ts:
-                keys_both(group, t, j)
-                keys_out(group, t, j)
-
-        turn_pair(x_turn, 0, 0)
-        out_pair("x", (0, 0), "vector")
-        turn_pair(x_turn, 0, 1)
+        x_turn(0, 0, 0)
+        x_turn(0, 0, 1)
+        turned_out("x", (0, 0), 0, "scalar")
+        x_turn(0, 1, 0)
+        turned_out("x", (0, 0), 1, "vector")
+        x_turn(0, 1, 1)
         x_quant(0, 0)
-        out_pair("x", (0, 1), "vector")
-        for c in range(4):
-            z_open(0, c)
-        z_passes(0, range(4), 0)
+        z_open(0, 0)
+        z_open(0, 1)
+        z_open(0, 2)
+        z_open(0, 3)
+        z_passes(0, [0, 1, 2, 3], 0)
+        x_turn(0, 2, 0)
+        turned_out("x", (0, 1), 0, "vector")
+        x_turn(0, 2, 1)
+        x_turn(0, 3, 0)
+        turned_out("x", (0, 1), 1, "scalar")
+        turned_out("x", (0, 2), 0, "scalar")
         x_quant(0, 1)
-        turn_pair(x_turn, 0, 2)
-        out_pair("x", (0, 2), "vector")
+        turned_out("x", (0, 2), 1, "scalar")
+        turned_out("x", (0, 3), 0, "vector")
+        x_turn(0, 3, 1)
+        z_passes(0, [0, 1, 2, 3], 1)
         x_quant(0, 2)
-        turn_pair(x_turn, 0, 3)
-        z_passes(0, range(4), 1)
-        out_pair("x", (0, 3), "vector")
-        z_passes(0, range(4), 2)
+        turned_out("x", (0, 3), 1, "vector")
+        z_passes(0, [0, 1, 2, 3], 2)
         x_quant(0, 3)
         z_passes(0, [0, 1], 3)
-        z_passes(0, [2, 3], 3)
-
-        wk_weave(0, 0, "vector")
-        z_all(0, [4, 5])
-        for c in range(4):
-            z_out(0, c)
-        turn_pair(x_turn, 1, 0)
-        turn_pair(x_turn, 1, 1)
+        wk_weave(0, 0, "scalar")
+        h_out(0, 0)
+        x_part(1, 0, "vector")
         wk_quant(0, 0)
-        out_pair("x", (1, 0))
-        v_quant(0, 0)
+        z_passes(0, [2, 3], 3)
+        h_out(0, 1)
+        h_out(0, 2)
+        x_part(1, 1, "vector")
+        z_all(0, [4])
+        v_out(0, 0)
+        h_out(0, 3)
+        x_turn(1, 0, 0)
+        x_turn(1, 0, 1)
+        v_out(0, 1)
+        v_out(0, 2)
+        turned_out("x", (1, 0), 0, "scalar")
+        v_out(0, 3)
+        x_turn(1, 1, 0)
+        h_out(0, 4)
+        turned_out("x", (1, 1), 0, "vector")
+        x_turn(1, 1, 1)
+        turned_out("x", (1, 1), 1, "scalar")
+        z_all(0, [5])
+        turned_out("x", (1, 0), 1, "scalar")
+        x_part(1, 2, "vector")
         wk_weave(1, 0, "vector")
+        x_part(1, 3, "scalar")
+        z_all(0, [6])
+        x_turn(1, 2, 0)
+        x_turn(1, 2, 1)
+        h_out(0, 5)
+        turned_out("x", (1, 2), 0, "scalar")
         x_quant(1, 0)
-        z_out(0, 4)
-        z_out(0, 5)
-        z_all(0, [6, 7])
-        out_pair("x", (1, 1))
-        wk_quant(1, 0)
-        wk_weave(0, 1, "vector")
+        v_out(0, 4)
+        x_turn(1, 3, 0)
+        turned_out("x", (1, 3), 0, "scalar")
+        x_turn(1, 3, 1)
+        h_turn(0, 0, 0)
         x_quant(1, 1)
-        turn_pair(x_turn, 1, 2)
-        turn_pair(x_turn, 1, 3)
-        out_pair("x", (1, 2))
-        wk_quant(0, 1)
-        z_out(0, 6)
+        h_turn(0, 0, 1)
+        z_all(0, [7])
+        turned_out("x", (1, 3), 1, "scalar")
+        turned_out("x", (1, 2), 1, "scalar")
+        v_quant(0, 0)
+        h_out(0, 6)
+        v_out(0, 5)
+        turned_out("h", (0, 0), 0, "vector")
+        mix_turn(0, 0)
+        h_out(0, 7)
+        turned_out("m", (0,), 0, "scalar")
         x_quant(1, 2)
-        out_pair("x", (1, 3))
-        z_out(0, 7)
-        turn_pair(h_turn, 0, 0)
+        turned_out("h", (0, 0), 1, "scalar")
+        mix_turn(0, 1)
+        turned_out("m", (0,), 1, "scalar")
+        h_turn(0, 1, 0)
         x_quant(1, 3)
-        wk_weave(1, 1, "vector")
-        out_pair("h", (0, 0))
-        v_quant(0, 1)
-        z_all(1, [0, 1])
-        wk_quant(1, 1)
-        turn_pair(h_turn, 0, 1)
+        wk_quant(1, 0)
+        h_turn(0, 1, 1)
+        turned_out("h", (0, 1), 0, "vector")
+        v_out(0, 6)
         h_quant(0, 0)
-        out_pair("h", (0, 1))
-        z_out(1, 0)
+        turned_out("h", (0, 1), 1, "scalar")
+        wk_weave(0, 1, "scalar")
+        z_all(1, [0])
+        z_all(1, [1])
         h_quant(0, 1)
-        z_out(1, 1)
-        wk_weave(0, 2, "scalar")
-        z_all(1, [2, 3])
-        keys_run(0, 0, range(2))
-        z_out(1, 2)
-        z_out(1, 3)
-        keys_run(0, 0, range(2, 4))
-        wk_quant(0, 2)
-        wk_weave(1, 2, "scalar")
-        keys_run(0, 1, range(2))
-        v_quant(1, 0)
-        turn_pair(mix_turn, 0)
-        turn_pair(mix_turn, 1)
-        out_pair("m", (0,))
-        keys_run(0, 1, range(2, 4))
-        wk_quant(1, 2)
-        z_all(1, [4, 5])
+        v_out(0, 7)
+        v_out(1, 0)
+        keys_both(0, 0, 0)
+        keys_both(0, 1, 0)
+        keys_out(0, 0, 0)
+        z_all(1, [2])
+        keys_both(0, 2, 0)
         mix_quant(0)
-        out_pair("m", (1,))
-        keys_run(0, 2, range(2))
+        keys_out(0, 1, 0)
+        keys_both(0, 3, 0)
+        v_out(1, 1)
+        mix_turn(1, 0)
+        wk_weave(1, 1, "scalar")
+        keys_out(0, 2, 0)
+        keys_out(0, 3, 0)
+        wk_quant(0, 1)
+        mix_turn(1, 1)
+        h_out(1, 0)
+        turned_out("m", (1,), 0, "scalar")
+        wk_quant(1, 1)
+        z_all(1, [3])
+        h_out(1, 1)
+        v_quant(0, 1)
+        turned_out("m", (1,), 1, "scalar")
+        keys_both(0, 0, 1)
+        v_out(1, 2)
+        wk_weave(0, 2, "scalar")
+        keys_out(0, 0, 1)
+        keys_both(0, 1, 1)
+        keys_both(0, 2, 1)
+        keys_out(0, 1, 1)
+        keys_out(0, 2, 1)
+        v_out(1, 3)
+        h_out(1, 2)
+        keys_both(0, 3, 1)
+        keys_out(0, 3, 1)
+        z_all(1, [4])
+        z_all(1, [5])
+        v_quant(1, 0)
         mix_quant(1)
-        turn_pair(h_turn, 1, 0)
-        z_out(1, 4)
-        z_out(1, 5)
-        out_pair("h", (1, 0))
+        v_out(1, 4)
+        slots_both(0, 0)
+        h_out(1, 3)
+        slots_both(1, 0)
+        slots_out(0, 0)
         z_all(1, [6])
-        keys_run(0, 2, range(2, 4))
         z_all(1, [7])
-        z_out(1, 6)
+        wk_weave(1, 2, "scalar")
+        slots_out(1, 0)
+        v_out(1, 5)
+        wk_quant(0, 2)
+        slots_both(2, 0)
+        h_out(1, 4)
+        v_out(1, 6)
+        wk_quant(1, 2)
+        slots_both(3, 0)
+        keys_both(0, 0, 2)
+        h_out(1, 5)
+        h_turn(1, 0, 0)
+        h_out(1, 6)
+        v_out(1, 7)
+        h_out(1, 7)
+        h_turn(1, 0, 1)
+        slots_out(2, 0)
+        h_turn(1, 1, 0)
+        v_quant(1, 1)
+        turned_out("h", (1, 0), 0, "scalar")
+        h_turn(1, 1, 1)
+        slots_out(3, 0)
+        slots_both(0, 1)
+        slots_both(1, 1)
+        turned_out("h", (1, 0), 1, "scalar")
+        keys_out(0, 0, 2)
         h_quant(1, 0)
-        z_out(1, 7)
-        for s in range(4):
-            slots_both(s, 0)
-            slots_out(s, 0)
-            if s == 1:
-                v_quant(1, 1)
-        turn_pair(h_turn, 1, 1)
-        out_pair("h", (1, 1))
-        for s in range(4):
-            slots_both(s, 1)
-            slots_out(s, 1)
-            if s == 1:
-                h_quant(1, 1)
-        for j in range(3):
-            keys_run(1, j, range(4))
+        slots_out(0, 1)
+        slots_out(1, 1)
+        turned_out("h", (1, 1), 0, "scalar")
+        turned_out("h", (1, 1), 1, "scalar")
+        slots_both(2, 1)
+        slots_out(2, 1)
+        slots_both(3, 1)
+        h_quant(1, 1)
+        keys_both(0, 1, 2)
+        keys_both(0, 2, 2)
+        keys_both(0, 3, 2)
+        keys_out(0, 1, 2)
+        keys_out(0, 2, 2)
+        keys_out(0, 3, 2)
+        keys_both(1, 0, 0)
+        keys_both(1, 0, 1)
+        keys_both(1, 0, 2)
+        keys_out(1, 0, 0)
+        keys_both(1, 1, 0)
+        keys_out(1, 0, 1)
+        keys_both(1, 1, 1)
+        keys_both(1, 1, 2)
+        keys_out(1, 0, 2)
+        keys_both(1, 2, 0)
+        keys_both(1, 2, 1)
+        keys_out(1, 1, 0)
+        keys_out(1, 1, 1)
+        slots_out(3, 1)
+        keys_out(1, 1, 2)
+        keys_both(1, 2, 2)
+        keys_out(1, 2, 0)
+        keys_out(1, 2, 1)
+        keys_out(1, 2, 2)
+        keys_both(1, 3, 0)
+        keys_both(1, 3, 1)
+        keys_both(1, 3, 2)
+        keys_out(1, 3, 0)
+        keys_out(1, 3, 1)
+        keys_out(1, 3, 2)

@@ -63,7 +63,6 @@ def tile_text_image_bridge_s9_kernel(
         nc.vector.memset(w_plane[1][:].bitcast(I32), 0)
         ident = kept("ident", 0, [P, P], F32)
         make_identity(nc, ident[:])
-        nc.scalar.activation(out=warm[:, 4:8], in_=warm[:, 0:4], func=RELU)
 
         x_sb, w_sb, wk_raw, mix_sb = {}, {}, {}, {}
 
@@ -109,31 +108,34 @@ def tile_text_image_bridge_s9_kernel(
             nc.sync.dma_start(out=tile[:, cols], in_=row[cols].partition_broadcast(P))
 
         emph = kept("emph", 0, [P, 2, PACK], BF16)
+        bias_cols = kept("bias_cols", 0, [P, 3, PACK], BF16)
+        bias_f32 = kept("bias_f32", 0, [P, 3 * PACK], F32)
         bias = kept("bias", 0, [P, D], BF16)
         gains = kept("gains", 0, [P, F], BF16)
 
+        nc.scalar.dma_start(out=bias_cols[:], in_=b_key.rearrange("(j p c) -> p j c", j=3, c=PACK))
+        nc.scalar.dma_start(out=emph[:], in_=emphasis.rearrange("(g p t) -> p g t", g=2, t=PACK))
+        nc.scalar.activation(out=warm[:, 4:8], in_=warm[:, 0:4], func=RELU)
         load_x(0, 0, pieces=2)
         load_x(0, 1)
         load_w(0)
         load_x(0, 2)
         load_x(0, 3)
-        load_wk(0, 0, 1)
-        load_w(1)
         load_x(1, 0)
         load_x(1, 1)
-        nc.sync.dma_start(out=emph[:], in_=emphasis.rearrange("(g p t) -> p g t", g=2, t=PACK))
-        load_x(1, 3)
+        load_wk(0, 0, 1)
+        load_w(1)
         load_x(1, 2)
         load_wk(1, 0, 1)
+        load_x(1, 3)
         load_mix(0)
-        load_mix(1)
-        load_row(bias, b_key, 0)
         load_wk(0, 1, 3)
-        load_row(bias, b_key, 2)
+        load_mix(1)
         load_wk(1, 1, 3)
         load_row(gains, gain, 0)
         load_row(gains, gain, 1)
-        load_row(bias, b_key, 1)
+
+        nc.vector.tensor_copy(out=bias_f32[:], in_=bias_cols[:].rearrange("p j c -> p (j c)"))
 
         banks = {}
         staged = {}
@@ -159,6 +161,22 @@ def tile_text_image_bridge_s9_kernel(
 
         def mix_part(pair, engine="scalar"):
             part(("m", pair), mix_sb[pair][:].rearrange("p s k -> p (s k)"), engine)
+
+        def bias_turn(j):
+            number, bank = take_bank()
+            banks["b", j] = number, bank
+            for c in range(PACK):
+                column = bias_f32[:, PACK * j + c : PACK * j + c + 1]
+                nc.tensor.transpose(bank[:, c * P : (c + 1) * P], column.to_broadcast([P, P]), ident[:])
+
+        def bias_out(j, engine):
+            number, bank = banks.pop(("b", j))
+            copy_on(
+                engine,
+                bias[:, j * KP : (j + 1) * KP].rearrange("p (n c) -> p n c", c=PACK),
+                bank[:].rearrange("p (c n) -> p n c", c=PACK),
+            )
+            free_banks.append(number)
 
         def x_turn(group, t, half):
             number, bank = take_bank()
@@ -295,13 +313,39 @@ def tile_text_image_bridge_s9_kernel(
                 stop=(g == 1),
             )
 
-        def keys_out(group, t, j):
+        late_stores = []
+
+        def finish(bank, result, row, op, engine):
+            if engine == "vector":
+                nc.vector.tensor_tensor(out=result, in0=bank[:], in1=row, op=op)
+            else:
+                nc.scalar.copy(out=result, in_=bank[:])
+                nc.gpsimd.tensor_tensor(out=result, in0=result, in1=row, op=op)
+
+        def store(out, result, engine):
+            for entry in late_stores:
+                entry[2] += 1
+            if out is not None and engine == "vector":
+                nc.sync.dma_start(out=out, in_=result)
+            elif out is not None:
+                late_stores.append([out, result, 0])
+            while late_stores and late_stores[0][2] >= 2:
+                entry = late_stores.pop(0)
+                nc.sync.dma_start(out=entry[0], in_=entry[1])
+
+        def keys_out(group, t, j, engine="vector"):
             number, bank = banks.pop(("k", group, t, j))
-            result = stage.tile([P, KP], F32, name="result", tag="result", bufs=12)
             cols = slice(j * KP, (j + 1) * KP)
-            nc.vector.tensor_tensor(out=result[:], in0=bank[:], in1=bias[:, cols], op=ALU.add)
             rows = keys[group * KP : (group + 1) * KP, :].rearrange("(p t) d -> p t d", t=PACK)
-            nc.sync.dma_start(out=rows[:, t, cols], in_=result[:])
+            if group == 1 and t < 3:
+                if j == 0:
+                    staged["wide"] = stage.tile([P, D], F32, name="wide", bufs=3)
+                finish(bank, staged["wide"][:, cols], bias[:, cols], ALU.add, engine)
+                store(rows[:, t, :] if j == 2 else None, staged["wide"][:], "vector")
+            else:
+                result = stage.tile([P, KP], F32, name="result", tag="result", bufs=7)
+                finish(bank, result[:], bias[:, cols], ALU.add, engine)
+                store(rows[:, t, cols], result[:], engine)
             free_banks.append(number)
 
         def keys_both(group, t, j):
@@ -323,218 +367,225 @@ def tile_text_image_bridge_s9_kernel(
                     stop=(group == 1),
                 )
 
-        def slots_out(s, h):
+        def slots_out(s, h, engine="vector"):
             number, bank = banks.pop(("s", s, h))
-            result = stage.tile([P, KP], F32, name="result", tag="result", bufs=12)
+            result = stage.tile([P, KP], F32, name="result", tag="result", bufs=7)
             cols = slice(h * KP, (h + 1) * KP)
-            nc.vector.tensor_tensor(out=result[:], in0=bank[:], in1=gains[:, cols], op=ALU.mult)
-            nc.sync.dma_start(out=slots[s * P : (s + 1) * P, cols], in_=result[:])
+            finish(bank, result[:], gains[:, cols], ALU.mult, engine)
+            store(slots[s * P : (s + 1) * P, cols], result[:], engine)
             free_banks.append(number)
 
         x_turn(0, 0, 0)
+        turned_out("x", (0, 0), 0, "vector")
         x_turn(0, 0, 1)
-        turned_out("x", (0, 0), 0, "scalar")
-        x_turn(0, 1, 0)
-        turned_out("x", (0, 0), 1, "vector")
-        x_turn(0, 1, 1)
+        bias_turn(0)
+        turned_out("x", (0, 0), 1, "scalar")
+        bias_out(0, "scalar")
         x_quant(0, 0)
+        x_turn(0, 1, 0)
+        x_turn(0, 1, 1)
+        bias_turn(1)
+        bias_turn(2)
+        turned_out("x", (0, 1), 0, "scalar")
         z_open(0, 0)
         z_open(0, 1)
         z_open(0, 2)
         z_open(0, 3)
         z_passes(0, [0, 1, 2, 3], 0)
         x_turn(0, 2, 0)
-        turned_out("x", (0, 1), 0, "vector")
+        turned_out("x", (0, 1), 1, "scalar")
+        bias_out(1, "scalar")
+        bias_out(2, "scalar")
+        turned_out("x", (0, 2), 0, "scalar")
         x_turn(0, 2, 1)
         x_turn(0, 3, 0)
-        turned_out("x", (0, 1), 1, "scalar")
-        turned_out("x", (0, 2), 0, "scalar")
         x_quant(0, 1)
+        x_part(1, 0, "vector")
         turned_out("x", (0, 2), 1, "scalar")
-        turned_out("x", (0, 3), 0, "vector")
         x_turn(0, 3, 1)
+        turned_out("x", (0, 3), 0, "vector")
+        turned_out("x", (0, 3), 1, "scalar")
         z_passes(0, [0, 1, 2, 3], 1)
         x_quant(0, 2)
-        turned_out("x", (0, 3), 1, "vector")
-        z_passes(0, [0, 1, 2, 3], 2)
         x_quant(0, 3)
+        z_passes(0, [0, 1, 2, 3], 2)
+        x_part(1, 1, "scalar")
         z_passes(0, [0, 1], 3)
-        wk_weave(0, 0, "scalar")
         h_out(0, 0)
-        x_part(1, 0, "vector")
-        wk_quant(0, 0)
         z_passes(0, [2, 3], 3)
-        h_out(0, 1)
-        h_out(0, 2)
-        x_part(1, 1, "vector")
         z_all(0, [4])
-        v_out(0, 0)
-        h_out(0, 3)
+        h_out(0, 1)
         x_turn(1, 0, 0)
+        wk_weave(0, 0, "vector")
+        wk_quant(0, 0)
+        v_out(0, 0)
         x_turn(1, 0, 1)
-        v_out(0, 1)
-        v_out(0, 2)
-        turned_out("x", (1, 0), 0, "scalar")
-        v_out(0, 3)
         x_turn(1, 1, 0)
+        v_out(0, 1)
+        x_part(1, 2, "vector")
+        x_turn(1, 1, 1)
+        h_out(0, 2)
+        h_out(0, 3)
+        z_all(0, [5])
+        v_out(0, 2)
+        z_all(0, [6])
+        turned_out("x", (1, 0), 0, "scalar")
+        turned_out("x", (1, 0), 1, "scalar")
         h_out(0, 4)
         turned_out("x", (1, 1), 0, "vector")
-        x_turn(1, 1, 1)
-        turned_out("x", (1, 1), 1, "scalar")
-        z_all(0, [5])
-        turned_out("x", (1, 0), 1, "scalar")
-        x_part(1, 2, "vector")
-        wk_weave(1, 0, "vector")
-        x_part(1, 3, "scalar")
-        z_all(0, [6])
         x_turn(1, 2, 0)
+        x_part(1, 3, "scalar")
+        turned_out("x", (1, 1), 1, "scalar")
+        v_out(0, 3)
         x_turn(1, 2, 1)
-        h_out(0, 5)
-        turned_out("x", (1, 2), 0, "scalar")
-        x_quant(1, 0)
-        v_out(0, 4)
+        wk_weave(1, 0, "vector")
         x_turn(1, 3, 0)
-        turned_out("x", (1, 3), 0, "scalar")
         x_turn(1, 3, 1)
+        h_out(0, 5)
         h_turn(0, 0, 0)
-        x_quant(1, 1)
+        v_out(0, 4)
+        turned_out("x", (1, 2), 0, "scalar")
+        turned_out("x", (1, 2), 1, "scalar")
+        x_quant(1, 0)
+        h_out(0, 6)
+        turned_out("x", (1, 3), 0, "scalar")
+        wk_quant(1, 0)
         h_turn(0, 0, 1)
         z_all(0, [7])
-        turned_out("x", (1, 3), 1, "scalar")
-        turned_out("x", (1, 2), 1, "scalar")
-        v_quant(0, 0)
-        h_out(0, 6)
-        v_out(0, 5)
         turned_out("h", (0, 0), 0, "vector")
+        turned_out("x", (1, 3), 1, "scalar")
         mix_turn(0, 0)
+        x_quant(1, 1)
         h_out(0, 7)
-        turned_out("m", (0,), 0, "scalar")
         x_quant(1, 2)
-        turned_out("h", (0, 0), 1, "scalar")
+        v_out(0, 5)
         mix_turn(0, 1)
-        turned_out("m", (0,), 1, "scalar")
-        h_turn(0, 1, 0)
         x_quant(1, 3)
-        wk_quant(1, 0)
-        h_turn(0, 1, 1)
-        turned_out("h", (0, 1), 0, "vector")
+        turned_out("h", (0, 0), 1, "scalar")
+        h_turn(0, 1, 0)
         v_out(0, 6)
-        h_quant(0, 0)
+        h_turn(0, 1, 1)
+        turned_out("h", (0, 1), 0, "scalar")
         turned_out("h", (0, 1), 1, "scalar")
-        wk_weave(0, 1, "scalar")
         z_all(1, [0])
         z_all(1, [1])
+        turned_out("m", (0,), 0, "scalar")
+        v_quant(0, 0)
+        h_quant(0, 0)
+        turned_out("m", (0,), 1, "scalar")
         h_quant(0, 1)
+        wk_weave(0, 1, "scalar")
         v_out(0, 7)
-        v_out(1, 0)
         keys_both(0, 0, 0)
         keys_both(0, 1, 0)
-        keys_out(0, 0, 0)
-        z_all(1, [2])
-        keys_both(0, 2, 0)
-        mix_quant(0)
-        keys_out(0, 1, 0)
-        keys_both(0, 3, 0)
-        v_out(1, 1)
-        mix_turn(1, 0)
         wk_weave(1, 1, "scalar")
-        keys_out(0, 2, 0)
-        keys_out(0, 3, 0)
-        wk_quant(0, 1)
-        mix_turn(1, 1)
-        h_out(1, 0)
-        turned_out("m", (1,), 0, "scalar")
-        wk_quant(1, 1)
-        z_all(1, [3])
-        h_out(1, 1)
+        z_all(1, [2])
+        v_out(1, 0)
+        keys_both(0, 2, 0)
+        keys_out(0, 0, 0)
+        keys_both(0, 3, 0)
+        keys_out(0, 1, 0)
+        mix_turn(1, 0)
+        v_out(1, 1)
         v_quant(0, 1)
-        turned_out("m", (1,), 1, "scalar")
+        keys_out(0, 2, 0)
+        mix_turn(1, 1)
+        mix_quant(0)
+        wk_quant(0, 1)
+        z_all(1, [3])
+        wk_quant(1, 1)
+        h_out(1, 0)
         keys_both(0, 0, 1)
-        v_out(1, 2)
-        wk_weave(0, 2, "scalar")
-        keys_out(0, 0, 1)
         keys_both(0, 1, 1)
+        v_out(1, 2)
+        h_out(1, 1)
+        turned_out("m", (1,), 0, "scalar")
+        keys_out(0, 3, 0, "gpsimd")
         keys_both(0, 2, 1)
-        keys_out(0, 1, 1)
-        keys_out(0, 2, 1)
-        v_out(1, 3)
-        h_out(1, 2)
         keys_both(0, 3, 1)
-        keys_out(0, 3, 1)
+        v_out(1, 3)
+        keys_out(0, 0, 1)
+        keys_out(0, 1, 1)
         z_all(1, [4])
-        z_all(1, [5])
-        v_quant(1, 0)
-        mix_quant(1)
-        v_out(1, 4)
-        slots_both(0, 0)
+        h_out(1, 2)
+        keys_out(0, 2, 1)
+        turned_out("m", (1,), 1, "vector")
+        wk_weave(0, 2, "scalar")
         h_out(1, 3)
+        v_quant(1, 0)
+        z_all(1, [5])
+        slots_both(0, 0)
         slots_both(1, 0)
-        slots_out(0, 0)
-        z_all(1, [6])
-        z_all(1, [7])
         wk_weave(1, 2, "scalar")
+        slots_out(0, 0, "gpsimd")
+        keys_out(0, 3, 1)
+        mix_quant(1)
+        z_all(1, [6])
+        v_out(1, 4)
         slots_out(1, 0)
         v_out(1, 5)
         wk_quant(0, 2)
-        slots_both(2, 0)
         h_out(1, 4)
-        v_out(1, 6)
+        slots_both(2, 0)
         wk_quant(1, 2)
-        slots_both(3, 0)
+        v_out(1, 6)
+        z_all(1, [7])
         keys_both(0, 0, 2)
-        h_out(1, 5)
-        h_turn(1, 0, 0)
-        h_out(1, 6)
+        keys_both(0, 1, 2)
+        slots_both(3, 0)
         v_out(1, 7)
+        h_turn(1, 0, 0)
+        keys_out(0, 0, 2)
+        h_out(1, 5)
+        h_out(1, 6)
         h_out(1, 7)
+        slots_out(2, 0, "gpsimd")
         h_turn(1, 0, 1)
-        slots_out(2, 0)
-        h_turn(1, 1, 0)
-        v_quant(1, 1)
         turned_out("h", (1, 0), 0, "scalar")
+        turned_out("h", (1, 0), 1, "scalar")
+        h_turn(1, 1, 0)
+        keys_out(0, 1, 2)
+        turned_out("h", (1, 1), 0, "scalar")
+        v_quant(1, 1)
         h_turn(1, 1, 1)
+        turned_out("h", (1, 1), 1, "scalar")
         slots_out(3, 0)
         slots_both(0, 1)
-        slots_both(1, 1)
-        turned_out("h", (1, 0), 1, "scalar")
-        keys_out(0, 0, 2)
         h_quant(1, 0)
         slots_out(0, 1)
-        slots_out(1, 1)
-        turned_out("h", (1, 1), 0, "scalar")
-        turned_out("h", (1, 1), 1, "scalar")
-        slots_both(2, 1)
-        slots_out(2, 1)
-        slots_both(3, 1)
+        slots_both(1, 1)
         h_quant(1, 1)
-        keys_both(0, 1, 2)
         keys_both(0, 2, 2)
+        slots_both(2, 1)
         keys_both(0, 3, 2)
-        keys_out(0, 1, 2)
-        keys_out(0, 2, 2)
-        keys_out(0, 3, 2)
+        slots_both(3, 1)
         keys_both(1, 0, 0)
+        slots_out(1, 1, "gpsimd")
+        keys_out(0, 2, 2)
         keys_both(1, 0, 1)
+        keys_out(0, 3, 2)
         keys_both(1, 0, 2)
-        keys_out(1, 0, 0)
+        keys_out(1, 0, 0, "gpsimd")
+        slots_out(2, 1)
         keys_both(1, 1, 0)
+        slots_out(3, 1)
         keys_out(1, 0, 1)
         keys_both(1, 1, 1)
-        keys_both(1, 1, 2)
         keys_out(1, 0, 2)
+        keys_both(1, 1, 2)
         keys_both(1, 2, 0)
-        keys_both(1, 2, 1)
-        keys_out(1, 1, 0)
+        keys_out(1, 1, 0, "gpsimd")
         keys_out(1, 1, 1)
-        slots_out(3, 1)
+        keys_both(1, 2, 1)
         keys_out(1, 1, 2)
-        keys_both(1, 2, 2)
-        keys_out(1, 2, 0)
+        keys_out(1, 2, 0, "gpsimd")
         keys_out(1, 2, 1)
-        keys_out(1, 2, 2)
+        keys_both(1, 2, 2)
         keys_both(1, 3, 0)
         keys_both(1, 3, 1)
         keys_both(1, 3, 2)
+        keys_out(1, 2, 2)
         keys_out(1, 3, 0)
         keys_out(1, 3, 1)
         keys_out(1, 3, 2)
+        assert not late_stores

@@ -108,34 +108,32 @@ def tile_text_image_bridge_s9_kernel(
             nc.sync.dma_start(out=tile[:, cols], in_=row[cols].partition_broadcast(P))
 
         emph = kept("emph", 0, [P, 2, PACK], BF16)
-        bias_cols = kept("bias_cols", 0, [P, 3, PACK], BF16)
-        bias_f32 = kept("bias_f32", 0, [P, 3 * PACK], F32)
         bias = kept("bias", 0, [P, D], BF16)
         gains = kept("gains", 0, [P, F], BF16)
 
-        nc.scalar.dma_start(out=bias_cols[:], in_=b_key.rearrange("(j p c) -> p j c", j=3, c=PACK))
-        nc.scalar.dma_start(out=emph[:], in_=emphasis.rearrange("(g p t) -> p g t", g=2, t=PACK))
         nc.scalar.activation(out=warm[:, 4:8], in_=warm[:, 0:4], func=RELU)
         load_x(0, 0, pieces=2)
         load_x(0, 1)
         load_w(0)
         load_x(0, 2)
         load_x(0, 3)
+        load_w(1)
+        load_wk(0, 0, 1)
         load_x(1, 0)
         load_x(1, 1)
-        load_wk(0, 0, 1)
-        load_w(1)
+        nc.sync.dma_start(out=emph[:], in_=emphasis.rearrange("(g p t) -> p g t", g=2, t=PACK))
         load_x(1, 2)
-        load_wk(1, 0, 1)
         load_x(1, 3)
+        load_wk(1, 0, 1)
+        load_row(bias, b_key, 0)
         load_mix(0)
         load_wk(0, 1, 3)
-        load_mix(1)
         load_wk(1, 1, 3)
+        load_row(bias, b_key, 1)
+        load_mix(1)
         load_row(gains, gain, 0)
+        load_row(bias, b_key, 2)
         load_row(gains, gain, 1)
-
-        nc.vector.tensor_copy(out=bias_f32[:], in_=bias_cols[:].rearrange("p j c -> p (j c)"))
 
         banks = {}
         staged = {}
@@ -143,40 +141,24 @@ def tile_text_image_bridge_s9_kernel(
 
         parted = {}
 
-        def part(index, rows, engine):
+        def part(index, rows, engine, pieces=1):
             parted[index] = stage.tile([P, 8, P], F32, name="parted", bufs=3, align_bytes=64)
-            copy_on(
-                engine,
-                parted[index][:].rearrange("p (a u) m -> p a u m", u=2),
-                rows.bitcast(F32).rearrange("p (a m u) -> p a u m", m=P, u=2),
-            )
+            out = parted[index][:].rearrange("p (a u) m -> p a u m", u=2)
+            in_ = rows.bitcast(F32).rearrange("p (a m u) -> p a u m", m=P, u=2)
+            step = 4 // pieces
+            for a in range(0, 4, step):
+                copy_on(engine, out[:, a : a + step], in_[:, a : a + step])
 
         def word_column(index, rows, i):
             if index in parted:
                 return parted[index][:, i, :]
             return rows.bitcast(F32)[:, 256 * (i // 2) + i % 2 : 256 * (i // 2 + 1) : 2]
 
-        def x_part(group, t, engine="scalar"):
-            part(("x", group, t), x_sb[group, t][:], engine)
+        def x_part(group, t, engine="scalar", pieces=1):
+            part(("x", group, t), x_sb[group, t][:], engine, pieces)
 
         def mix_part(pair, engine="scalar"):
             part(("m", pair), mix_sb[pair][:].rearrange("p s k -> p (s k)"), engine)
-
-        def bias_turn(j):
-            number, bank = take_bank()
-            banks["b", j] = number, bank
-            for c in range(PACK):
-                column = bias_f32[:, PACK * j + c : PACK * j + c + 1]
-                nc.tensor.transpose(bank[:, c * P : (c + 1) * P], column.to_broadcast([P, P]), ident[:])
-
-        def bias_out(j, engine):
-            number, bank = banks.pop(("b", j))
-            copy_on(
-                engine,
-                bias[:, j * KP : (j + 1) * KP].rearrange("p (n c) -> p n c", c=PACK),
-                bank[:].rearrange("p (c n) -> p n c", c=PACK),
-            )
-            free_banks.append(number)
 
         def x_turn(group, t, half):
             number, bank = take_bank()
@@ -375,217 +357,215 @@ def tile_text_image_bridge_s9_kernel(
             store(slots[s * P : (s + 1) * P, cols], result[:], engine)
             free_banks.append(number)
 
+        x_part(0, 0, "vector", pieces=2)
+        x_part(0, 1, "vector")
         x_turn(0, 0, 0)
-        turned_out("x", (0, 0), 0, "vector")
+        turned_out("x", (0, 0), 0, "scalar")
         x_turn(0, 0, 1)
-        bias_turn(0)
         turned_out("x", (0, 0), 1, "scalar")
-        bias_out(0, "scalar")
         x_quant(0, 0)
         x_turn(0, 1, 0)
         x_turn(0, 1, 1)
-        bias_turn(1)
-        bias_turn(2)
         turned_out("x", (0, 1), 0, "scalar")
+        turned_out("x", (0, 1), 1, "vector")
+        x_quant(0, 1)
+        x_part(0, 2, "vector")
         z_open(0, 0)
         z_open(0, 1)
         z_open(0, 2)
         z_open(0, 3)
         z_passes(0, [0, 1, 2, 3], 0)
+        x_part(0, 3, "vector")
         x_turn(0, 2, 0)
-        turned_out("x", (0, 1), 1, "scalar")
-        bias_out(1, "scalar")
-        bias_out(2, "scalar")
-        turned_out("x", (0, 2), 0, "scalar")
         x_turn(0, 2, 1)
         x_turn(0, 3, 0)
-        x_quant(0, 1)
-        x_part(1, 0, "vector")
-        turned_out("x", (0, 2), 1, "scalar")
+        turned_out("x", (0, 2), 0, "vector")
         x_turn(0, 3, 1)
         turned_out("x", (0, 3), 0, "vector")
+        turned_out("x", (0, 2), 1, "scalar")
         turned_out("x", (0, 3), 1, "scalar")
-        z_passes(0, [0, 1, 2, 3], 1)
         x_quant(0, 2)
+        z_passes(0, [0, 1, 2, 3], 1)
         x_quant(0, 3)
         z_passes(0, [0, 1, 2, 3], 2)
-        x_part(1, 1, "scalar")
         z_passes(0, [0, 1], 3)
         h_out(0, 0)
-        z_passes(0, [2, 3], 3)
-        z_all(0, [4])
         h_out(0, 1)
-        x_turn(1, 0, 0)
         wk_weave(0, 0, "vector")
-        wk_quant(0, 0)
-        v_out(0, 0)
-        x_turn(1, 0, 1)
-        x_turn(1, 1, 0)
-        v_out(0, 1)
-        x_part(1, 2, "vector")
-        x_turn(1, 1, 1)
+        z_passes(0, [2, 3], 3)
         h_out(0, 2)
+        z_all(0, [4])
         h_out(0, 3)
+        x_part(1, 0, "vector")
+        wk_quant(0, 0)
+        x_part(1, 1, "vector")
+        x_turn(1, 0, 0)
+        x_turn(1, 0, 1)
+        v_out(0, 0)
+        v_out(0, 1)
+        x_turn(1, 1, 0)
+        turned_out("x", (1, 0), 0, "scalar")
+        h_out(0, 4)
+        turned_out("x", (1, 0), 1, "scalar")
+        x_part(1, 2, "vector")
+        turned_out("x", (1, 1), 0, "vector")
+        x_part(1, 3, "scalar")
+        x_turn(1, 1, 1)
         z_all(0, [5])
         v_out(0, 2)
         z_all(0, [6])
-        turned_out("x", (1, 0), 0, "scalar")
-        turned_out("x", (1, 0), 1, "scalar")
-        h_out(0, 4)
-        turned_out("x", (1, 1), 0, "vector")
         x_turn(1, 2, 0)
-        x_part(1, 3, "scalar")
-        turned_out("x", (1, 1), 1, "scalar")
-        v_out(0, 3)
-        x_turn(1, 2, 1)
-        wk_weave(1, 0, "vector")
-        x_turn(1, 3, 0)
-        x_turn(1, 3, 1)
         h_out(0, 5)
-        h_turn(0, 0, 0)
-        v_out(0, 4)
+        v_out(0, 3)
+        turned_out("x", (1, 1), 1, "scalar")
+        x_turn(1, 2, 1)
         turned_out("x", (1, 2), 0, "scalar")
-        turned_out("x", (1, 2), 1, "scalar")
-        x_quant(1, 0)
-        h_out(0, 6)
+        v_out(0, 4)
+        x_turn(1, 3, 0)
         turned_out("x", (1, 3), 0, "scalar")
-        wk_quant(1, 0)
+        x_turn(1, 3, 1)
+        x_quant(1, 0)
+        wk_weave(1, 0, "vector")
+        h_turn(0, 0, 0)
+        turned_out("x", (1, 2), 1, "scalar")
         h_turn(0, 0, 1)
-        z_all(0, [7])
-        turned_out("h", (0, 0), 0, "vector")
         turned_out("x", (1, 3), 1, "scalar")
+        z_all(0, [7])
+        h_out(0, 6)
         mix_turn(0, 0)
-        x_quant(1, 1)
         h_out(0, 7)
-        x_quant(1, 2)
-        v_out(0, 5)
         mix_turn(0, 1)
-        x_quant(1, 3)
+        turned_out("h", (0, 0), 0, "vector")
         turned_out("h", (0, 0), 1, "scalar")
         h_turn(0, 1, 0)
-        v_out(0, 6)
-        h_turn(0, 1, 1)
-        turned_out("h", (0, 1), 0, "scalar")
-        turned_out("h", (0, 1), 1, "scalar")
-        z_all(1, [0])
-        z_all(1, [1])
+        x_quant(1, 1)
+        x_quant(1, 2)
         turned_out("m", (0,), 0, "scalar")
-        v_quant(0, 0)
+        x_quant(1, 3)
+        h_turn(0, 1, 1)
+        v_out(0, 5)
+        z_all(1, [0])
         h_quant(0, 0)
-        turned_out("m", (0,), 1, "scalar")
+        turned_out("h", (0, 1), 0, "scalar")
+        z_all(1, [1])
+        v_out(0, 6)
+        wk_quant(1, 0)
+        turned_out("h", (0, 1), 1, "scalar")
         h_quant(0, 1)
-        wk_weave(0, 1, "scalar")
         v_out(0, 7)
+        v_quant(0, 0)
         keys_both(0, 0, 0)
+        turned_out("m", (0,), 1, "scalar")
         keys_both(0, 1, 0)
-        wk_weave(1, 1, "scalar")
+        wk_weave(0, 1, "scalar")
         z_all(1, [2])
-        v_out(1, 0)
-        keys_both(0, 2, 0)
         keys_out(0, 0, 0)
+        mix_quant(0)
+        v_out(1, 0)
+        wk_weave(1, 1, "scalar")
+        keys_both(0, 2, 0)
         keys_both(0, 3, 0)
         keys_out(0, 1, 0)
         mix_turn(1, 0)
         v_out(1, 1)
-        v_quant(0, 1)
-        keys_out(0, 2, 0)
-        mix_turn(1, 1)
-        mix_quant(0)
-        wk_quant(0, 1)
-        z_all(1, [3])
-        wk_quant(1, 1)
         h_out(1, 0)
-        keys_both(0, 0, 1)
-        keys_both(0, 1, 1)
-        v_out(1, 2)
+        wk_quant(0, 1)
+        mix_turn(1, 1)
         h_out(1, 1)
         turned_out("m", (1,), 0, "scalar")
+        z_all(1, [3])
+        wk_quant(1, 1)
+        keys_both(0, 0, 1)
+        keys_both(0, 1, 1)
+        keys_out(0, 2, 0)
         keys_out(0, 3, 0, "gpsimd")
         keys_both(0, 2, 1)
-        keys_both(0, 3, 1)
-        v_out(1, 3)
-        keys_out(0, 0, 1)
+        keys_out(0, 0, 1, "gpsimd")
+        v_quant(0, 1)
+        v_out(1, 2)
         keys_out(0, 1, 1)
-        z_all(1, [4])
+        keys_both(0, 3, 1)
         h_out(1, 2)
         keys_out(0, 2, 1)
+        v_out(1, 3)
+        z_all(1, [4])
         turned_out("m", (1,), 1, "vector")
-        wk_weave(0, 2, "scalar")
-        h_out(1, 3)
-        v_quant(1, 0)
         z_all(1, [5])
+        v_quant(1, 0)
+        wk_weave(0, 2, "scalar")
         slots_both(0, 0)
         slots_both(1, 0)
-        wk_weave(1, 2, "scalar")
-        slots_out(0, 0, "gpsimd")
-        keys_out(0, 3, 1)
+        v_out(1, 4)
         mix_quant(1)
         z_all(1, [6])
-        v_out(1, 4)
+        slots_out(0, 0)
         slots_out(1, 0)
-        v_out(1, 5)
         wk_quant(0, 2)
-        h_out(1, 4)
         slots_both(2, 0)
+        wk_weave(1, 2, "scalar")
         wk_quant(1, 2)
-        v_out(1, 6)
+        h_out(1, 3)
+        slots_out(2, 0, "gpsimd")
         z_all(1, [7])
+        v_out(1, 5)
+        v_out(1, 6)
+        h_out(1, 4)
         keys_both(0, 0, 2)
         keys_both(0, 1, 2)
-        slots_both(3, 0)
-        v_out(1, 7)
-        h_turn(1, 0, 0)
-        keys_out(0, 0, 2)
         h_out(1, 5)
         h_out(1, 6)
+        slots_both(3, 0)
+        v_out(1, 7)
+        keys_out(0, 3, 1)
         h_out(1, 7)
-        slots_out(2, 0, "gpsimd")
+        h_turn(1, 0, 0)
+        keys_out(0, 0, 2, "gpsimd")
         h_turn(1, 0, 1)
         turned_out("h", (1, 0), 0, "scalar")
-        turned_out("h", (1, 0), 1, "scalar")
         h_turn(1, 1, 0)
-        keys_out(0, 1, 2)
-        turned_out("h", (1, 1), 0, "scalar")
         v_quant(1, 1)
+        keys_out(0, 1, 2)
         h_turn(1, 1, 1)
-        turned_out("h", (1, 1), 1, "scalar")
+        turned_out("h", (1, 0), 1, "scalar")
+        turned_out("h", (1, 1), 0, "scalar")
         slots_out(3, 0)
         slots_both(0, 1)
-        h_quant(1, 0)
         slots_out(0, 1)
         slots_both(1, 1)
-        h_quant(1, 1)
         keys_both(0, 2, 2)
+        slots_out(1, 1)
+        turned_out("h", (1, 1), 1, "scalar")
         slots_both(2, 1)
         keys_both(0, 3, 2)
         slots_both(3, 1)
-        keys_both(1, 0, 0)
-        slots_out(1, 1, "gpsimd")
-        keys_out(0, 2, 2)
-        keys_both(1, 0, 1)
-        keys_out(0, 3, 2)
-        keys_both(1, 0, 2)
-        keys_out(1, 0, 0, "gpsimd")
+        h_quant(1, 0)
+        keys_out(0, 2, 2, "gpsimd")
+        h_quant(1, 1)
         slots_out(2, 1)
-        keys_both(1, 1, 0)
         slots_out(3, 1)
+        keys_both(1, 0, 0)
+        keys_out(1, 0, 0, "gpsimd")
+        keys_both(1, 0, 1)
+        keys_both(1, 0, 2)
+        keys_both(1, 1, 0)
+        keys_out(0, 3, 2)
         keys_out(1, 0, 1)
-        keys_both(1, 1, 1)
         keys_out(1, 0, 2)
-        keys_both(1, 1, 2)
-        keys_both(1, 2, 0)
         keys_out(1, 1, 0, "gpsimd")
+        keys_both(1, 1, 1)
+        keys_both(1, 1, 2)
         keys_out(1, 1, 1)
-        keys_both(1, 2, 1)
+        keys_both(1, 2, 0)
         keys_out(1, 1, 2)
+        keys_both(1, 2, 1)
         keys_out(1, 2, 0, "gpsimd")
-        keys_out(1, 2, 1)
         keys_both(1, 2, 2)
+        keys_out(1, 2, 1)
         keys_both(1, 3, 0)
-        keys_both(1, 3, 1)
-        keys_both(1, 3, 2)
         keys_out(1, 2, 2)
+        keys_both(1, 3, 1)
         keys_out(1, 3, 0)
+        keys_both(1, 3, 2)
         keys_out(1, 3, 1)
         keys_out(1, 3, 2)
         assert not late_stores

from contextlib import ExitStack

import concourse.mybir as mybir
from concourse.masks import make_identity

T, C, F, D, Q = 1024, 2048, 1024, 1536, 512
FLOPS = 2 * T * C * F + 2 * T * F * D + 2 * Q * T * F

F32 = mybir.dt.float32
BF16 = mybir.dt.bfloat16
I32 = mybir.dt.int32
U32 = mybir.dt.uint32
U8 = mybir.dt.uint8
E4M3 = mybir.dt.float8_e4m3fn_x4
E5M2 = mybir.dt.float8_e5m2_x4
E2M1 = mybir.dt.float4_e2m1fn_x4
ALU = mybir.AluOpType
RELU = mybir.ActivationFunctionType.Relu

P = 128
PACK = 4
KP = P * PACK
BANKS = 8


def tile_text_image_bridge_s9_kernel(
    tc, x, w_words, w_scales, w_key, b_key, emphasis, mix, gain, keys, slots
):
    nc = tc.nc
    with ExitStack() as ctx:
        keep = ctx.enter_context(tc.tile_pool(name="keep", bufs=1))
        stage = ctx.enter_context(tc.tile_pool(name="stage", bufs=2))
        psum = ctx.enter_context(tc.psum_pool(name="psum", bufs=1))
        ctx.enter_context(tc.manual_schedule())

        def kept(name, index, shape, dtype):
            return keep.tile(shape, dtype, name="%s_%s" % (name, index), align_bytes=64)

        free_banks = list(range(BANKS))

        def take_bank():
            number = free_banks.pop(0)
            bank = psum.tile([P, KP], F32, name="bank%d" % number, tag="bank%d" % number)
            return number, bank

        def quantize(name, index, source, fmt):
            width = source.shape[1] // PACK
            codes = kept(name + "_codes", index, [P, width], U32)
            scales = kept(name + "_scales", index, [P, width], U8)
            nc.vector.quantize_mx(out=codes[:].bitcast(fmt), scales=scales[:], in_=source)
            return codes, scales

        def copy_on(engine, out, in_):
            if engine == "scalar":
                nc.scalar.copy(out=out, in_=in_)
            else:
                nc.vector.tensor_copy(out=out, in_=in_)

        w_plane = [kept("w_plane", h, [P, 4, KP], U8) for h in range(2)]
        warm = kept("warm", 0, [P, 8], F32)
        nc.vector.memset(w_plane[0][:].bitcast(I32), 0)
        nc.vector.memset(warm[:, 0:4], 0.0)
        nc.vector.memset(w_plane[1][:].bitcast(I32), 0)
        ident = kept("ident", 0, [P, P], F32)
        make_identity(nc, ident[:])

        x_sb, w_sb, wk_raw, mix_sb = {}, {}, {}, {}

        def load_x(group, t, pieces=1):
            x_sb[group, t] = kept("x", 4 * group + t, [P, C], BF16)
            rows = x[group * KP : (group + 1) * KP, :].rearrange("(p t) k -> p t k", t=PACK)
            step = C // pieces
            for k0 in range(0, C, step):
                nc.sync.dma_start(out=x_sb[group, t][:, k0 : k0 + step], in_=rows[:, t, k0 : k0 + step])

        def load_w(h):
            for quad in range(4):
                nc.sync.dma_start(
                    out=w_plane[h][32 * quad : 32 * quad + 4, :, :].bitcast(I32),
                    in_=w_scales[:, 4 * quad : 4 * quad + 4, h * KP : (h + 1) * KP]
                    .rearrange("g r n -> r g n")
                    .bitcast(I32),
                )
            w_sb[h] = kept("w", h, [P, 4, 2 * KP], U8)
            nc.sync.dma_start(
                out=w_sb[h][:].bitcast(I32),
                in_=w_words[:, :, 2 * h * KP : 2 * (h + 1) * KP].rearrange("g p n -> p g n").bitcast(I32),
            )

        def load_wk(g, first, last):
            raw = kept("wk_raw", 3 * g + first, [P, PACK, (last - first) * KP], BF16)
            nc.sync.dma_start(
                out=raw[:],
                in_=w_key[g * KP : (g + 1) * KP, first * KP : last * KP].rearrange("(p t) d -> p t d", t=PACK),
            )
            for j in range(first, last):
                wk_raw[g, j] = raw[:, :, (j - first) * KP : (j - first + 1) * KP]

        def load_mix(pair):
            mix_sb[pair] = kept("mix", pair, [P, 2, T], BF16)
            nc.sync.dma_start(
                out=mix_sb[pair][:],
                in_=mix[2 * pair * P : 2 * (pair + 1) * P, :].rearrange("(s p) k -> p s k", p=P),
            )

        def load_row(tile, row, j):
            cols = slice(j * KP, (j + 1) * KP)
            nc.sync.dma_start(out=tile[:, cols], in_=row[cols].partition_broadcast(P))

        emph = kept("emph", 0, [P, 2, PACK], BF16)
        bias = kept("bias", 0, [P, D], BF16)
        gains = kept("gains", 0, [P, F], BF16)

        nc.scalar.activation(out=warm[:, 4:8], in_=warm[:, 0:4], func=RELU)
        load_x(0, 0, pieces=2)
        load_x(0, 1)
        load_w(0)
        load_x(0, 2)
        load_x(0, 3)
        load_w(1)
        load_wk(0, 0, 1)
        load_x(1, 0)
        load_x(1, 1)
        nc.sync.dma_start(out=emph[:], in_=emphasis.rearrange("(g p t) -> p g t", g=2, t=PACK))
        load_x(1, 2)
        load_x(1, 3)
        load_wk(1, 0, 1)
        load_row(bias, b_key, 0)
        load_mix(0)
        load_wk(0, 1, 3)
        load_wk(1, 1, 3)
        load_row(bias, b_key, 1)
        load_mix(1)
        load_row(gains, gain, 0)
        load_row(bias, b_key, 2)
        load_row(gains, gain, 1)

        banks = {}
        staged = {}
        xq, hq, vq, wq, mq = {}, {}, {}, {}, {}

        parted = {}

        def part(index, rows, engine, pieces=1):
            parted[index] = stage.tile([P, 8, P], F32, name="parted", bufs=3, align_bytes=64)
            out = parted[index][:].rearrange("p (a u) m -> p a u m", u=2)
            in_ = rows.bitcast(F32).rearrange("p (a m u) -> p a u m", m=P, u=2)
            step = 4 // pieces
            for a in range(0, 4, step):
                copy_on(engine, out[:, a : a + step], in_[:, a : a + step])

        def word_column(index, rows, i):
            if index in parted:
                return parted[index][:, i, :]
            return rows.bitcast(F32)[:, 256 * (i // 2) + i % 2 : 256 * (i // 2 + 1) : 2]

        def x_part(group, t, engine="scalar", pieces=1):
            part(("x", group, t), x_sb[group, t][:], engine, pieces)

        def mix_part(pair, engine="scalar"):
            part(("m", pair), mix_sb[pair][:].rearrange("p s k -> p (s k)"), engine)

        def x_turn(group, t, half):
            number, bank = take_bank()
            banks["x", group, t, half] = number, bank
            for i in range(4):
                nc.tensor.transpose(
                    bank[:, i * P : (i + 1) * P], word_column(("x", group, t), x_sb[group, t][:], 4 * half + i), ident[:]
                )

        def turned_out(kind, index, half, engine):
            number, bank = banks.pop((kind,) + index + (half,))
            if half == 0:
                staged[kind, index] = stage.tile(
                    [P, 4 * KP], BF16, name="turned_" + kind, tag="turned", bufs=4, align_bytes=64
                )
            out = staged[kind, index][:, half * 2 * KP : (half + 1) * 2 * KP].bitcast(F32)
            copy_on(
                engine,
                out.rearrange("p (a r u) -> p a r u", a=2, u=2),
                bank[:].rearrange("p (a u r) -> p a r u", a=2, u=2),
            )
            free_banks.append(number)

        def x_quant(group, t):
            xq[group, t] = quantize("x", 4 * group + t, staged.pop(("x", (group, t)))[:], E4M3)

        def z_open(group, c):
            banks["z", group, c] = take_bank()

        def z_passes(group, chunks, t):
            codes, scales = xq[group, t]
            for g in range(4):
                for c in chunks:
                    h, cc = divmod(c, 4)
                    nc.tensor.matmul_mx(
                        out=banks["z", group, c][1][:, t * P : (t + 1) * P],
                        lhsT=codes[:, g * P : (g + 1) * P].bitcast(E4M3),
                        lhsT_scale=scales[:, g * P : (g + 1) * P],
                        rhs=w_sb[h][:, g, 2 * cc * P : 2 * (cc + 1) * P].bitcast(E2M1),
                        rhs_scale=w_plane[h][:, g, cc * P : (cc + 1) * P],
                        start=(g == 0),
                        stop=(g == 3),
                    )

        def z_all(group, chunks):
            for c in chunks:
                z_open(group, c)
            for t in range(PACK):
                z_passes(group, chunks, t)

        z_read = set()

        def z_release(group, c):
            if (group, c) in z_read:
                free_banks.append(banks.pop(("z", group, c))[0])
            z_read.add((group, c))

        def h_out(group, c):
            bank = banks["z", group, c][1]
            h, cc = divmod(c, 4)
            if cc == 0:
                staged["h", group, h] = stage.tile([P, PACK, 2, 256], BF16, name="h_rows", bufs=3, align_bytes=64)
            nc.scalar.activation(
                out=staged["h", group, h][:, :, :, 64 * cc : 64 * (cc + 1)].rearrange("p t u (m e) -> p u t m e", e=2),
                in_=bank[:].rearrange("p (t m u e) -> p u t m e", t=PACK, u=2, e=2),
                func=RELU,
            )
            z_release(group, c)

        def v_out(group, c):
            bank = banks["z", group, c][1]
            h, cc = divmod(c, 4)
            if cc == 0:
                staged["v", group, h] = stage.tile([P, KP, PACK], BF16, name="v_rows", bufs=2, align_bytes=64)
            nc.vector.scalar_tensor_tensor(
                out=staged["v", group, h][:, cc * P : (cc + 1) * P, :],
                in0=bank[:].rearrange("p (t f) -> p f t", t=PACK),
                scalar=0.0,
                in1=emph[:, group, :].unsqueeze(1).to_broadcast([P, P, PACK]),
                op0=ALU.max,
                op1=ALU.mult,
            )
            z_release(group, c)

        def z_out(group, c):
            h_out(group, c)
            v_out(group, c)

        def v_quant(group, h):
            rows = staged.pop(("v", group, h))
            vq[group, h] = quantize("v", 2 * group + h, rows[:].rearrange("p f t -> p (f t)"), E5M2)

        def h_turn(group, g, half):
            number, bank = take_bank()
            banks["h", group, g, half] = number, bank
            words = staged["h", group, g][:].bitcast(F32)
            for i in range(4):
                nc.tensor.transpose(bank[:, i * P : (i + 1) * P], words[:, 2 * half + i // 2, i % 2, :], ident[:])

        def h_quant(group, g):
            hq[group, g] = quantize("h", 2 * group + g, staged.pop(("h", (group, g)))[:], E5M2)

        def mix_turn(pair, half):
            number, bank = take_bank()
            banks["m", pair, half] = number, bank
            for i in range(4):
                nc.tensor.transpose(bank[:, i * P : (i + 1) * P], word_column(("m", pair), mix_sb[pair][:].rearrange("p s k -> p (s k)"), 4 * half + i), ident[:])

        def mix_quant(pair):
            mq[pair] = quantize("mix", pair, staged.pop(("m", (pair,)))[:], E4M3)

        def wk_weave(g, j, engine):
            staged["wk", g, j] = stage.tile([P, KP, PACK], BF16, name="wk_rows", bufs=2, align_bytes=64)
            copy_on(
                engine,
                staged["wk", g, j][:].rearrange("p (c i) t -> p c t i", i=4),
                wk_raw[g, j].rearrange("p t (c i) -> p c t i", i=4),
            )

        def wk_quant(g, j):
            rows = staged.pop(("wk", g, j))
            wq[g, j] = quantize("wk", 3 * g + j, rows[:].rearrange("p d t -> p (d t)"), E4M3)

        def keys_pass(group, t, j, g):
            if g == 0:
                banks["k", group, t, j] = take_bank()
            nc.tensor.matmul_mx(
                out=banks["k", group, t, j][1][:],
                lhsT=hq[group, g][0][:, t * P : (t + 1) * P].bitcast(E5M2),
                lhsT_scale=hq[group, g][1][:, t * P : (t + 1) * P],
                rhs=wq[g, j][0][:].bitcast(E4M3),
                rhs_scale=wq[g, j][1][:],
                start=(g == 0),
                stop=(g == 1),
            )

        late_stores = []

        def finish(bank, result, row, op, engine):
            if engine == "vector":
                nc.vector.tensor_tensor(out=result, in0=bank[:], in1=row, op=op)
            else:
                nc.scalar.copy(out=result, in_=bank[:])
                nc.gpsimd.tensor_tensor(out=result, in0=result, in1=row, op=op)

        def store(out, result, engine):
            for entry in late_stores:
                entry[2] += 1
            if out is not None and engine == "vector":
                nc.sync.dma_start(out=out, in_=result)
            elif out is not None:
                late_stores.append([out, result, 0])
            while late_stores and late_stores[0][2] >= 2:
                entry = late_stores.pop(0)
                nc.sync.dma_start(out=entry[0], in_=entry[1])

        def keys_out(group, t, j, engine="vector"):
            number, bank = banks.pop(("k", group, t, j))
            cols = slice(j * KP, (j + 1) * KP)
            rows = keys[group * KP : (group + 1) * KP, :].rearrange("(p t) d -> p t d", t=PACK)
            if group == 1 and t < 3:
                if j == 0:
                    staged["wide"] = stage.tile([P, D], F32, name="wide", bufs=3)
                finish(bank, staged["wide"][:, cols], bias[:, cols], ALU.add, engine)
                store(rows[:, t, :] if j == 2 else None, staged["wide"][:], "vector")
            else:
                result = stage.tile([P, KP], F32, name="result", tag="result", bufs=7)
                finish(bank, result[:], bias[:, cols], ALU.add, engine)
                store(rows[:, t, cols], result[:], engine)
            free_banks.append(number)

        def keys_both(group, t, j):
            keys_pass(group, t, j, 0)
            keys_pass(group, t, j, 1)

        def slots_both(s, h):
            banks["s", s, h] = take_bank()
            codes, scales = mq[s // 2]
            for group in range(2):
                cols = slice((2 * (s % 2) + group) * P, (2 * (s % 2) + group + 1) * P)
                nc.tensor.matmul_mx(
                    out=banks["s", s, h][1][:],
                    lhsT=codes[:, cols].bitcast(E4M3),
                    lhsT_scale=scales[:, cols],
                    rhs=vq[group, h][0][:].bitcast(E5M2),
                    rhs_scale=vq[group, h][1][:],
                    start=(group == 0),
                    stop=(group == 1),
                )

        def slots_out(s, h, engine="vector"):
            number, bank = banks.pop(("s", s, h))
            result = stage.tile([P, KP], F32, name="result", tag="result", bufs=7)
            cols = slice(h * KP, (h + 1) * KP)
            finish(bank, result[:], gains[:, cols], ALU.mult, engine)
            store(slots[s * P : (s + 1) * P, cols], result[:], engine)
            free_banks.append(number)

        x_part(0, 0, "vector", pieces=2)
        x_part(0, 1, "vector")
        x_turn(0, 0, 0)
        turned_out("x", (0, 0), 0, "scalar")
        x_turn(0, 0, 1)
        turned_out("x", (0, 0), 1, "scalar")
        x_quant(0, 0)
        x_turn(0, 1, 0)
        x_turn(0, 1, 1)
        turned_out("x", (0, 1), 0, "scalar")
        turned_out("x", (0, 1), 1, "vector")
        x_quant(0, 1)
        x_part(0, 2, "vector")
        z_open(0, 0)
        z_open(0, 1)
        z_open(0, 2)
        z_open(0, 3)
        z_passes(0, [0, 1, 2, 3], 0)
        x_part(0, 3, "vector")
        x_turn(0, 2, 0)
        x_turn(0, 2, 1)
        x_turn(0, 3, 0)
        turned_out("x", (0, 2), 0, "vector")
        x_turn(0, 3, 1)
        turned_out("x", (0, 3), 0, "vector")
        turned_out("x", (0, 2), 1, "scalar")
        turned_out("x", (0, 3), 1, "scalar")
        x_quant(0, 2)
        z_passes(0, [0, 1, 2, 3], 1)
        x_quant(0, 3)
        z_passes(0, [0, 1, 2, 3], 2)
        z_passes(0, [0, 1], 3)
        h_out(0, 0)
        h_out(0, 1)
        wk_weave(0, 0, "vector")
        z_passes(0, [2, 3], 3)
        h_out(0, 2)
        z_all(0, [4])
        h_out(0, 3)
        x_part(1, 0, "vector")
        wk_quant(0, 0)
        x_part(1, 1, "vector")
        x_turn(1, 0, 0)
        x_turn(1, 0, 1)
        v_out(0, 0)
        v_out(0, 1)
        x_turn(1, 1, 0)
        turned_out("x", (1, 0), 0, "scalar")
        h_out(0, 4)
        turned_out("x", (1, 0), 1, "scalar")
        x_part(1, 2, "vector")
        turned_out("x", (1, 1), 0, "vector")
        x_part(1, 3, "scalar")
        x_turn(1, 1, 1)
        z_all(0, [5])
        v_out(0, 2)
        z_all(0, [6])
        x_turn(1, 2, 0)
        h_out(0, 5)
        v_out(0, 3)
        turned_out("x", (1, 1), 1, "scalar")
        x_turn(1, 2, 1)
        turned_out("x", (1, 2), 0, "scalar")
        v_out(0, 4)
        x_turn(1, 3, 0)
        turned_out("x", (1, 3), 0, "scalar")
        x_turn(1, 3, 1)
        x_quant(1, 0)
        wk_weave(1, 0, "vector")
        h_turn(0, 0, 0)
        turned_out("x", (1, 2), 1, "scalar")
        h_turn(0, 0, 1)
        turned_out("x", (1, 3), 1, "scalar")
        z_all(0, [7])
        h_out(0, 6)
        mix_turn(0, 0)
        h_out(0, 7)
        mix_turn(0, 1)
        turned_out("h", (0, 0), 0, "vector")
        turned_out("h", (0, 0), 1, "scalar")
        h_turn(0, 1, 0)
        x_quant(1, 1)
        x_quant(1, 2)
        turned_out("m", (0,), 0, "scalar")
        x_quant(1, 3)
        h_turn(0, 1, 1)
        v_out(0, 5)
        z_all(1, [0])
        h_quant(0, 0)
        turned_out("h", (0, 1), 0, "scalar")
        z_all(1, [1])
        v_out(0, 6)
        wk_quant(1, 0)
        turned_out("h", (0, 1), 1, "scalar")
        h_quant(0, 1)
        v_out(0, 7)
        v_quant(0, 0)
        keys_both(0, 0, 0)
        turned_out("m", (0,), 1, "scalar")
        keys_both(0, 1, 0)
        wk_weave(0, 1, "scalar")
        z_all(1, [2])
        keys_out(0, 0, 0)
        mix_quant(0)
        v_out(1, 0)
        wk_weave(1, 1, "scalar")
        keys_both(0, 2, 0)
        keys_both(0, 3, 0)
        keys_out(0, 1, 0)
        mix_turn(1, 0)
        v_out(1, 1)
        h_out(1, 0)
        wk_quant(0, 1)
        mix_turn(1, 1)
        h_out(1, 1)
        turned_out("m", (1,), 0, "scalar")
        z_all(1, [3])
        wk_quant(1, 1)
        keys_both(0, 0, 1)
        keys_both(0, 1, 1)
        keys_out(0, 2, 0)
        keys_out(0, 3, 0, "gpsimd")
        keys_both(0, 2, 1)
        keys_out(0, 0, 1, "gpsimd")
        v_quant(0, 1)
        v_out(1, 2)
        keys_out(0, 1, 1)
        keys_both(0, 3, 1)
        h_out(1, 2)
        keys_out(0, 2, 1)
        v_out(1, 3)
        z_all(1, [4])
        turned_out("m", (1,), 1, "vector")
        z_all(1, [5])
        v_quant(1, 0)
        wk_weave(0, 2, "scalar")
        slots_both(0, 0)
        slots_both(1, 0)
        v_out(1, 4)
        mix_quant(1)
        z_all(1, [6])
        slots_out(0, 0)
        slots_out(1, 0)
        wk_quant(0, 2)
        slots_both(2, 0)
        wk_weave(1, 2, "scalar")
        wk_quant(1, 2)
        h_out(1, 3)
        slots_out(2, 0, "gpsimd")
        z_all(1, [7])
        v_out(1, 5)
        v_out(1, 6)
        h_out(1, 4)
        keys_both(0, 0, 2)
        keys_both(0, 1, 2)
        h_out(1, 5)
        h_out(1, 6)
        slots_both(3, 0)
        v_out(1, 7)
        keys_out(0, 3, 1)
        h_out(1, 7)
        h_turn(1, 0, 0)
        keys_out(0, 0, 2, "gpsimd")
        h_turn(1, 0, 1)
        turned_out("h", (1, 0), 0, "scalar")
        h_turn(1, 1, 0)
        v_quant(1, 1)
        keys_out(0, 1, 2)
        h_turn(1, 1, 1)
        turned_out("h", (1, 0), 1, "scalar")
        turned_out("h", (1, 1), 0, "scalar")
        slots_out(3, 0)
        slots_both(0, 1)
        slots_out(0, 1)
        slots_both(1, 1)
        keys_both(0, 2, 2)
        slots_out(1, 1)
        turned_out("h", (1, 1), 1, "scalar")
        slots_both(2, 1)
        keys_both(0, 3, 2)
        slots_both(3, 1)
        h_quant(1, 0)
        keys_out(0, 2, 2, "gpsimd")
        h_quant(1, 1)
        slots_out(2, 1)
        slots_out(3, 1)
        keys_both(1, 0, 0)
        keys_out(1, 0, 0, "gpsimd")
        keys_both(1, 0, 1)
        keys_both(1, 0, 2)
        keys_both(1, 1, 0)
        keys_out(0, 3, 2)
        keys_out(1, 0, 1)
        keys_out(1, 0, 2)
        keys_out(1, 1, 0, "gpsimd")
        keys_both(1, 1, 1)
        keys_both(1, 1, 2)
        keys_out(1, 1, 1)
        keys_both(1, 2, 0)
        keys_out(1, 1, 2)
        keys_both(1, 2, 1)
        keys_out(1, 2, 0, "gpsimd")
        keys_both(1, 2, 2)
        keys_out(1, 2, 1)
        keys_both(1, 3, 0)
        keys_out(1, 2, 2)
        keys_both(1, 3, 1)
        keys_out(1, 3, 0)
        keys_both(1, 3, 2)
        keys_out(1, 3, 1)
        keys_out(1, 3, 2)
        assert not late_stores
